import numpy as np
import ml_dtypes


def mxq(x, axis, fmt="e4m3"):
    dtype, down = {"e4m3": (ml_dtypes.float8_e4m3fn, 7), "e5m2": (ml_dtypes.float8_e5m2, 14)}[fmt]
    v = np.moveaxis(np.asarray(x, np.float32).astype(ml_dtypes.bfloat16).astype(np.float64), axis, -1)
    blocks = v.reshape(v.shape[:-1] + (-1, 32))
    amax = np.abs(blocks).max(-1, keepdims=True)
    byte = np.maximum(np.where(amax > 0, np.frexp(amax)[1] - 1 + 127, 0) - down, 1)
    scale = np.exp2(byte - 127.0)
    codes = (blocks / scale).astype(np.float32).astype(dtype).astype(np.float64)
    return np.moveaxis((codes * scale).reshape(v.shape), -1, axis)


WIDE = False


def mx_kscale(k):
    if not WIDE:
        return np.ones(k)
    levels = np.array([10, -10, 5, -5, 0])
    if k % 512:
        return np.exp2(np.random.permutation(np.resize(levels, k // 32))).repeat(32)
    a = np.empty((k // 512, 16))
    for p in range(k // 512):
        a[p, :8] = np.random.permutation(np.resize(levels, 8))
        for g in range(8):
            far = levels[np.abs(levels - a[p, g]) >= 10]
            a[p, g + 8] = far[np.random.randint(len(far))]
    return np.exp2(a.ravel()).repeat(32)


def f64(x):
    return np.asarray(x).astype(np.float64)


def striped(idx):
    return np.tile(idx.reshape(-1, 16).T, (8, 1)).astype(np.uint16)


def unstriped(offs):
    return offs[:16].T.reshape(-1).astype(np.int64)


def striped8(idx):
    return np.concatenate([x.reshape(-1, 16).T for x in idx]).astype(np.uint16)


def runs(offs, k):
    lists = np.stack([offs[16 * r : 16 * r + 16].T.reshape(-1) for r in range(8)]).astype(np.int64)
    return lists[np.arange(k) % 512 // 64]


def pack_weight(w):
    k, n = w.shape
    w = f64(np.asarray(w, np.float32).astype(ml_dtypes.bfloat16)).reshape(k // 32, 32, n)
    amax = np.abs(w).max(1)
    byte = np.clip(np.where(amax > 0, np.frexp(amax)[1] - 1 + 127 - 7, 1), 1, 254)
    scaled = (w * np.exp2(127.0 - byte)[:, None, :]).reshape(k, n).astype(np.float32)
    words = np.ascontiguousarray(scaled.reshape(k // 512, 128, 4, n).transpose(0, 1, 3, 2)).astype(ml_dtypes.float8_e4m3fn).view(np.uint8)
    return words, np.ascontiguousarray(byte.astype(np.uint8).reshape(k // 512, 16, n))


def unpack_weight(words, scales):
    g, p, n, _ = words.shape
    vals = np.ascontiguousarray(words).view(ml_dtypes.float8_e4m3fn).astype(np.float64) * np.repeat(np.exp2(scales.astype(np.float64) - 127.0), 8, axis=1)[..., None]
    return vals.transpose(0, 1, 3, 2).reshape(g * 512, n)


def sigmoid(v):
    return 1.0 / (1.0 + np.exp(-np.maximum(v, -700.0)))


K, T, S, G, H, C = 512, 1024, 256, 2048, 512, 512


def setup_inputs():
    n = np.random.standard_normal
    s = mx_kscale(K)[:, None]
    packed_xT = pack_weight(n((K, T)) * s)
    packed_dT = pack_weight(n((K, G)) / s)
    return {
        "x_words": packed_xT[0],
        "x_scales": packed_xT[1],
        "d_words": packed_dT[0],
        "d_scales": packed_dT[1],
        "tau": np.random.uniform(0.3, 0.9, (H, 1)).astype(np.float32),
        "gs": (np.random.uniform(0.5, 1.5, (K, 1)) / s).astype(np.float32),
        "sl": np.random.uniform(1.0, 2.0, (H, 1)).astype(np.float32),
        "th": (0.5 * n((H, 1))).astype(np.float32),
        "offs": striped(np.random.permutation(T)[:S]),
        "k1": striped8(np.random.randint(0, G, (8, H))),
        "n1": striped(np.random.permutation(S)),
        "n2": striped(np.random.permutation(S)),
        "cand": striped(np.random.permutation(T)[:C]),
        "two": striped(np.random.permutation(T)[:S]),
        "k2": striped8(np.random.randint(0, G, (8, H))),
        "n3": striped(np.random.permutation(S)),
        "n4": striped(np.random.permutation(S)),
    }


def reference(x_words, x_scales, d_words, d_scales, tau, gs, sl, th, offs, k1, n1, n2, cand, two, k2, n3, n4):
    x_cand = unpack_weight(x_words, x_scales)[:, unstriped(cand)]
    d_k1 = unpack_weight(d_words, d_scales)[np.arange(K)[:, None], runs(k1, K)]
    xq = unpack_weight(x_words, x_scales)[:, unstriped(offs)]
    h = 0.0625 * (d_k1.T @ xq)
    low = h.min(axis=1, keepdims=True)
    ea = np.exp(f64(tau) * (low - h[:, unstriped(n1)]))
    z = f64(gs) * (h - (2.0 * (ea * h[:, unstriped(n2)])))
    a = 0.0625 * ((x_cand.T @ mxq(z, 0, "e4m3")))
    d_k2 = unpack_weight(d_words, d_scales)[np.arange(K)[:, None], runs(k2, K)]
    x_two = unpack_weight(x_words, x_scales)[:, unstriped(two)]
    b = 0.0625 * (d_k2.T @ x_two)
    sg = sigmoid(f64(sl) * (b[:, unstriped(n3)] - f64(th)))
    return a * sg - (0.5 * a[:, unstriped(n4)])

@@ -1,0 +1,192 @@
+from contextlib import ExitStack
+
+import concourse.mybir as mybir
+
+K, T, S, G, H, C = 512, 1024, 256, 2048, 512, 512
+FLOPS = 2 * K * S * (H + C + H)
+
+F32 = mybir.dt.float32
+BF16 = mybir.dt.bfloat16
+I32 = mybir.dt.int32
+U32 = mybir.dt.uint32
+U16 = mybir.dt.uint16
+U8 = mybir.dt.uint8
+FP8X4 = mybir.dt.float8_e4m3fn_x4
+ALU = mybir.AluOpType
+ACT = mybir.ActivationFunctionType
+
+P = 128
+PACK = 4
+TILES = H // P
+SIXTEENTH = 0.0625
+
+
+def tile_picked_pqcjgxbebz_none_p_kernel(
+    tc, x_words, x_scales, d_words, d_scales, tau, gs, sl, th, offs, k1, n1, n2, cand, two, k2, n3, n4, out
+):
+    nc = tc.nc
+    with ExitStack() as ctx:
+        keep = ctx.enter_context(tc.tile_pool(name="keep", bufs=1))
+        psum = ctx.enter_context(tc.psum_pool(name="psum", bufs=1))
+
+        def load_list(name, src):
+            tile = keep.tile(list(src.shape), U16, name=name)
+            nc.sync.dma_start(tile[:], src)
+            return tile
+
+        d_bytes = keep.tile([P, G], U8, name="d_bytes", align_bytes=64)
+        x_bytes = keep.tile([P, T], U8, name="x_bytes", align_bytes=64)
+        nc.vector.memset(d_bytes[:].bitcast(I32), 0)
+        nc.vector.memset(x_bytes[:].bitcast(I32), 0)
+        d_rows = d_scales[0].bitcast(I32)
+        x_rows = x_scales[0].bitcast(I32)
+        k1_t = load_list("k1_t", k1)
+        k2_t = load_list("k2_t", k2)
+        for e in range(2):
+            nc.sync.dma_start(d_bytes[:].bitcast(I32)[e:P:16, :], d_rows[e:16:2, :])
+
+        def load_x_rows(q):
+            nc.sync.dma_start(x_bytes[:].bitcast(I32)[32 * q : 32 * q + 4, :], x_rows[4 * q : 4 * q + 4, :])
+
+        for q in range(3):
+            load_x_rows(q)
+        d_codes = keep.tile([P, G], I32, name="d_codes", align_bytes=64)
+        nc.sync.dma_start(d_codes[:], d_words[0].rearrange("p n t -> p (n t)").bitcast(I32))
+        load_x_rows(3)
+        offs_t = load_list("offs_t", offs)
+        tau_t = keep.tile([P, TILES], F32, name="tau_t")
+        nc.sync.dma_start(tau_t[:], tau.rearrange("(p t) o -> p (t o)", t=PACK))
+        n1_t = load_list("n1_t", n1)
+        x_codes = keep.tile([P, T], I32, name="x_codes", align_bytes=64)
+        nc.sync.dma_start(x_codes[:], x_words[0].rearrange("p n t -> p (n t)").bitcast(I32))
+        two_t = load_list("two_t", two)
+        n2_t = load_list("n2_t", n2)
+        cand_t = load_list("cand_t", cand)
+        n3_t = load_list("n3_t", n3)
+        n4_t = load_list("n4_t", n4)
+
+        def gather_words(name, table, offsets, n, tag):
+            tile = keep.tile([P, n], U32, name=name, tag=tag, align_bytes=64)
+            nc.vector.tensor_copy(tile[:], table[:].bitcast(U32).indirect(offsets[:]))
+            return tile
+
+        def gather_bytes(name, table, offsets, n, tag):
+            tile = keep.tile([P, n], U8, name=name, tag=tag, align_bytes=64)
+            nc.vector.tensor_copy(tile[:], table[:].indirect(offsets[:]))
+            return tile
+
+        def place_odd_rows(queue, dst, src):
+            for e in range(2):
+                queue.dma_start(dst[:].bitcast(I32)[2 + e : P : 32, :], src[:].bitcast(I32)[16 + e : P : 32, :])
+
+        def product(tag, lhs_words, lhs_bytes, t, rhs_words, rhs_bytes):
+            acc = psum.tile([P, S], F32, name="acc", tag=tag)
+            cols = slice(t * P, (t + 1) * P)
+            nc.tensor.matmul_mx(
+                out=acc[:],
+                lhsT=lhs_words[:, cols].bitcast(FP8X4),
+                lhsT_scale=lhs_bytes[:, cols],
+                rhs=rhs_words[:].bitcast(FP8X4),
+                rhs_scale=rhs_bytes[:],
+                start=True,
+                stop=True,
+            )
+            return acc
+
+        k1_bytes = gather_bytes("k1_bytes", d_bytes, k1_t, H, "k1_bytes")
+        k1_plane = keep.tile([P, H], U8, name="k1_plane", tag="lhs_bytes", align_bytes=64)
+        nc.vector.tensor_copy(
+            k1_plane[:].rearrange("p (t m) -> p t m", t=PACK), k1_bytes[:].rearrange("p (m t) -> p t m", t=PACK)
+        )
+        place_odd_rows(nc.scalar, k1_plane, k1_plane)
+        k1_words = gather_words("k1_words", d_codes, k1_t, H, "k1_words")
+        k1_dealt = keep.tile([P, H], U32, name="k1_dealt", tag="lhs_words", align_bytes=64)
+        nc.vector.tensor_copy(
+            k1_dealt[:].bitcast(I32).rearrange("p (t m) -> p t m", t=PACK),
+            k1_words[:].bitcast(I32).rearrange("p (m t) -> p t m", t=PACK),
+        )
+        offs_bytes = gather_bytes("offs_bytes", x_bytes, offs_t, S, "x_picked_bytes")
+        offs_words = gather_words("offs_words", x_codes, offs_t, S, "x_picked_words")
+
+        rows = keep.tile([P, 3, 8], F32, name="rows", tag="k1_words", align_bytes=64)
+        gs_t, sl_t, th_t = rows[:, 0, :TILES], rows[:, 1, :TILES], rows[:, 2, :TILES]
+        nc.sync.dma_start(gs_t, gs.rearrange("(p t) o -> p (t o)", t=PACK))
+        with nc.allow_non_contiguous_dma(reason="one value a row and partition"):
+            nc.sync.dma_start(sl_t, sl.rearrange("(t p) o -> p (t o)", p=P))
+            nc.sync.dma_start(th_t, th.rearrange("(t p) o -> p (t o)", p=P))
+
+        neg_tau = keep.tile([P, TILES], F32, name="neg_tau")
+        nc.scalar.activation(neg_tau[:], tau_t[:], ACT.Copy, scale=-1.0)
+
+        low = keep.tile([P, TILES], F32, name="low")
+        exp_bias = keep.tile([P, TILES], F32, name="exp_bias", tag="bias")
+        h, ea, h_n2 = [], [], []
+        for t in range(TILES):
+            col = slice(t, t + 1)
+            acc = product("bank%d" % t, k1_dealt, k1_plane, t, offs_words, offs_bytes)
+            h.append(keep.tile([P, 2 * S], F32, name="h%d" % t))
+            nc.vector.tensor_scalar(h[t][:, :S], acc[:], SIXTEENTH, None, ALU.mult, ALU.min, accum_out=low[:, col])
+            nc.vector.tensor_tensor(exp_bias[:, col], low[:, col], tau_t[:, col], ALU.mult)
+            ea.append(keep.tile([P, S], F32, name="ea%d" % t))
+            h_n2.append(keep.tile([P, S], F32, name="h_n2_%d" % t))
+            nc.scalar.activation(
+                ea[t][:], h[t][:].indirect(n1_t[:]), ACT.Exp, bias=exp_bias[:, col], scale=neg_tau[:, col]
+            )
+            nc.scalar.activation(h_n2[t][:], h[t][:].indirect(n2_t[:]), ACT.Copy, scale=-2.0)
+
+        sig_bias = keep.tile([P, TILES], F32, name="sig_bias", tag="bias")
+        nc.vector.scalar_tensor_tensor(sig_bias[:], sl_t, -1.0, th_t, ALU.mult, ALU.mult)
+
+        z = keep.tile([P, TILES, S], F32, name="z")
+        for t in range(TILES):
+            col = slice(t, t + 1)
+            pull = keep.tile([P, S], F32, name="pull%d" % t)
+            nc.vector.scalar_tensor_tensor(pull[:], h_n2[t][:], gs_t[:, col], ea[t][:], ALU.mult, ALU.mult)
+            nc.vector.scalar_tensor_tensor(z[:, t, :], h[t][:, :S], gs_t[:, col], pull[:], ALU.mult, ALU.add)
+
+        z_bf = keep.tile([P, S, PACK], BF16, name="z_bf", align_bytes=64)
+        nc.vector.tensor_copy(
+            z_bf[:].rearrange("p (c i) t -> p c t i", i=4), z[:].rearrange("p t (c i) -> p c t i", i=4)
+        )
+        z_words = keep.tile([P, S], U32, name="z_words", align_bytes=64)
+        z_bytes = keep.tile([P, S], U8, name="z_bytes", align_bytes=64)
+        nc.vector.quantize_mx(
+            out=z_words[:].bitcast(FP8X4), scales=z_bytes[:], in_=z_bf[:].rearrange("p j t -> p (j t)")
+        )
+
+        k2_bytes = gather_bytes("k2_bytes", d_bytes, k2_t, H, "k2_bytes")
+        k2_plane = keep.tile([P, H], U8, name="k2_plane", align_bytes=64)
+        nc.vector.tensor_copy(k2_plane[:].bitcast(I32), k2_bytes[:].bitcast(I32))
+        place_odd_rows(nc.sync, k2_plane, k2_bytes)
+        k2_words = gather_words("k2_words", d_codes, k2_t, H, "lhs_words")
+        two_bytes = gather_bytes("two_bytes", x_bytes, two_t, S, "x_picked_bytes")
+        two_words = gather_words("two_words", x_codes, two_t, S, "x_picked_words")
+        sg = []
+        for t in range(TILES):
+            col = slice(t, t + 1)
+            acc = product("bank%d" % (TILES + t), k2_words, k2_plane, t, two_words, two_bytes)
+            b = keep.tile([P, 2 * S], F32, name="b%d" % t)
+            nc.scalar.activation(b[:, :S], acc[:], ACT.Copy, scale=SIXTEENTH)
+            sg.append(keep.tile([P, S], F32, name="sg%d" % t))
+            nc.scalar.activation(
+                sg[t][:], b[:].indirect(n3_t[:]), ACT.Sigmoid, bias=sig_bias[:, col], scale=sl_t[:, col]
+            )
+
+        cand_bytes = gather_bytes("cand_bytes", x_bytes, cand_t, C, "lhs_bytes")
+        cand_words = gather_words("cand_words", x_codes, cand_t, C, "x_picked_words")
+        neg_half_a, gated = [], []
+        for t in range(TILES):
+            acc = product("bank%d" % t, cand_words, cand_bytes, t, z_words, z_bytes)
+            gated.append(keep.tile([P, S], F32, name="gated%d" % t))
+            nc.vector.scalar_tensor_tensor(gated[t][:], acc[:], SIXTEENTH, sg[t][:], ALU.mult, ALU.mult)
+            neg_half_a.append(keep.tile([P, 2 * S], F32, name="neg_half_a%d" % t))
+            nc.scalar.activation(neg_half_a[t][:, :S], acc[:], ACT.Copy, scale=-0.5 * SIXTEENTH)
+        for t in range(TILES):
+            res = keep.tile([P, S], F32, name="res%d" % t)
+            if t < TILES // 2:
+                nc.vector.tensor_tensor(res[:], neg_half_a[t][:].indirect(n4_t[:]), gated[t][:], ALU.add)
+            else:
+                fetched = keep.tile([P, S], F32, name="fetched%d" % t)
+                nc.scalar.activation(fetched[:], neg_half_a[t][:].indirect(n4_t[:]), ACT.Copy)
+                nc.vector.tensor_tensor(res[:], fetched[:], gated[t][:], ALU.add)
+            nc.sync.dma_start(out[t * P : (t + 1) * P, :], res[:])

@@ -37,55 +37,67 @@ def tile_picked_pqcjgxbebz_none_p_kernel(
         d_bytes = keep.tile([P, G], U8, name="d_bytes", align_bytes=64)
         x_bytes = keep.tile([P, T], U8, name="x_bytes", align_bytes=64)
         nc.vector.memset(d_bytes[:].bitcast(I32), 0)
-        nc.vector.memset(x_bytes[:].bitcast(I32), 0)
+        nc.gpsimd.memset(x_bytes[:].bitcast(I32), 0)
+        k2_plane = keep.tile([P, H], U8, name="k2_plane", align_bytes=64)
+        nc.vector.memset(k2_plane[:].bitcast(I32), 0)
         d_rows = d_scales[0].bitcast(I32)
         x_rows = x_scales[0].bitcast(I32)
-        k1_t = load_list("k1_t", k1)
-        k2_t = load_list("k2_t", k2)
-        for e in range(2):
-            nc.sync.dma_start(d_bytes[:].bitcast(I32)[e:P:16, :], d_rows[e:16:2, :])
 
         def load_x_rows(q):
             nc.sync.dma_start(x_bytes[:].bitcast(I32)[32 * q : 32 * q + 4, :], x_rows[4 * q : 4 * q + 4, :])
 
-        for q in range(3):
-            load_x_rows(q)
+        def load_column(name, src):
+            tile = keep.tile([P, TILES], F32, name=name)
+            nc.sync.dma_start(tile[:], src)
+            return tile
+
+        k1_t = load_list("k1_t", k1)
+        offs_t = load_list("offs_t", offs)
+        load_x_rows(0)
+        load_x_rows(1)
+        nc.sync.dma_start(d_bytes[:].bitcast(I32)[0:P:8, :], d_rows)
+        load_x_rows(2)
+        load_x_rows(3)
         d_codes = keep.tile([P, G], I32, name="d_codes", align_bytes=64)
         nc.sync.dma_start(d_codes[:], d_words[0].rearrange("p n t -> p (n t)").bitcast(I32))
-        load_x_rows(3)
-        offs_t = load_list("offs_t", offs)
-        tau_t = keep.tile([P, TILES], F32, name="tau_t")
-        nc.sync.dma_start(tau_t[:], tau.rearrange("(p t) o -> p (t o)", t=PACK))
-        n1_t = load_list("n1_t", n1)
+        k2_t = load_list("k2_t", k2)
         x_codes = keep.tile([P, T], I32, name="x_codes", align_bytes=64)
         nc.sync.dma_start(x_codes[:], x_words[0].rearrange("p n t -> p (n t)").bitcast(I32))
         two_t = load_list("two_t", two)
+        tau_t = load_column("tau_t", tau.rearrange("(p t) o -> p (t o)", t=PACK))
+        n1_t = load_list("n1_t", n1)
         n2_t = load_list("n2_t", n2)
+        gs_t = load_column("gs_t", gs.rearrange("(p t) o -> p (t o)", t=PACK))
         cand_t = load_list("cand_t", cand)
         n3_t = load_list("n3_t", n3)
+        with nc.allow_non_contiguous_dma(reason="one value a row and partition"):
+            sl_t = load_column("sl_t", sl.rearrange("(t p) o -> p (t o)", p=P))
+            th_t = load_column("th_t", th.rearrange("(t p) o -> p (t o)", p=P))
         n4_t = load_list("n4_t", n4)
 
         def gather_words(name, table, offsets, n, tag):
             tile = keep.tile([P, n], U32, name=name, tag=tag, align_bytes=64)
-            nc.vector.tensor_copy(tile[:], table[:].bitcast(U32).indirect(offsets[:]))
+            nc.vector.tensor_copy(tile[:], table[:].bitcast(U32).indirect(offsets))
             return tile
 
         def gather_bytes(name, table, offsets, n, tag):
             tile = keep.tile([P, n], U8, name=name, tag=tag, align_bytes=64)
-            nc.vector.tensor_copy(tile[:], table[:].indirect(offsets[:]))
+            nc.vector.tensor_copy(tile[:], table[:].indirect(offsets))
             return tile
 
-        def place_odd_rows(queue, dst, src):
-            for e in range(2):
-                queue.dma_start(dst[:].bitcast(I32)[2 + e : P : 32, :], src[:].bitcast(I32)[16 + e : P : 32, :])
+        def place_odd_rows(queue, dst, src, first):
+            for c in range(first, 4):
+                queue.dma_start(dst[:].bitcast(I32)[c:P:32, :], src[:].bitcast(I32)[8 * c : P : 32, :])
 
-        def product(tag, lhs_words, lhs_bytes, t, rhs_words, rhs_bytes):
+        def block(t):
+            return slice(t * P, (t + 1) * P)
+
+        def product(tag, lhs_words, lhs_bytes, rhs_words, rhs_bytes):
             acc = psum.tile([P, S], F32, name="acc", tag=tag)
-            cols = slice(t * P, (t + 1) * P)
             nc.tensor.matmul_mx(
                 out=acc[:],
-                lhsT=lhs_words[:, cols].bitcast(FP8X4),
-                lhsT_scale=lhs_bytes[:, cols],
+                lhsT=lhs_words.bitcast(FP8X4),
+                lhsT_scale=lhs_bytes,
                 rhs=rhs_words[:].bitcast(FP8X4),
                 rhs_scale=rhs_bytes[:],
                 start=True,
@@ -93,78 +105,77 @@ def tile_picked_pqcjgxbebz_none_p_kernel(
             )
             return acc
 
-        k1_bytes = gather_bytes("k1_bytes", d_bytes, k1_t, H, "k1_bytes")
+        k1_bytes = gather_bytes("k1_bytes", d_bytes, k1_t[:], H, "k1_bytes")
         k1_plane = keep.tile([P, H], U8, name="k1_plane", tag="lhs_bytes", align_bytes=64)
         nc.vector.tensor_copy(
             k1_plane[:].rearrange("p (t m) -> p t m", t=PACK), k1_bytes[:].rearrange("p (m t) -> p t m", t=PACK)
         )
-        place_odd_rows(nc.scalar, k1_plane, k1_plane)
-        k1_words = gather_words("k1_words", d_codes, k1_t, H, "k1_words")
+        place_odd_rows(nc.scalar, k1_plane, k1_plane, 1)
+        offs_bytes = gather_bytes("offs_bytes", x_bytes, offs_t[:], S, "x_picked_bytes")
+        k1_words = gather_words("k1_words", d_codes, k1_t[:], H, "k1_words")
+        offs_words = gather_words("offs_words", x_codes, offs_t[:], S, "x_picked_words")
         k1_dealt = keep.tile([P, H], U32, name="k1_dealt", tag="lhs_words", align_bytes=64)
         nc.vector.tensor_copy(
             k1_dealt[:].bitcast(I32).rearrange("p (t m) -> p t m", t=PACK),
             k1_words[:].bitcast(I32).rearrange("p (m t) -> p t m", t=PACK),
         )
-        offs_bytes = gather_bytes("offs_bytes", x_bytes, offs_t, S, "x_picked_bytes")
-        offs_words = gather_words("offs_words", x_codes, offs_t, S, "x_picked_words")
-
-        rows = keep.tile([P, 3, 8], F32, name="rows", tag="k1_words", align_bytes=64)
-        gs_t, sl_t, th_t = rows[:, 0, :TILES], rows[:, 1, :TILES], rows[:, 2, :TILES]
-        nc.sync.dma_start(gs_t, gs.rearrange("(p t) o -> p (t o)", t=PACK))
-        with nc.allow_non_contiguous_dma(reason="one value a row and partition"):
-            nc.sync.dma_start(sl_t, sl.rearrange("(t p) o -> p (t o)", p=P))
-            nc.sync.dma_start(th_t, th.rearrange("(t p) o -> p (t o)", p=P))
 
         neg_tau = keep.tile([P, TILES], F32, name="neg_tau")
         nc.scalar.activation(neg_tau[:], tau_t[:], ACT.Copy, scale=-1.0)
 
         low = keep.tile([P, TILES], F32, name="low")
-        exp_bias = keep.tile([P, TILES], F32, name="exp_bias", tag="bias")
+        exp_bias = keep.tile([P, TILES], F32, name="exp_bias")
         h, ea, h_n2 = [], [], []
+        h_sums = [
+            product("bank%d" % t, k1_dealt[:, block(t)], k1_plane[:, block(t)], offs_words, offs_bytes)
+            for t in range(TILES)
+        ]
         for t in range(TILES):
             col = slice(t, t + 1)
-            acc = product("bank%d" % t, k1_dealt, k1_plane, t, offs_words, offs_bytes)
+            if t == TILES // 2:
+                k2_bytes = gather_bytes("k2_bytes", d_bytes, k2_t[:], H, "lhs_bytes")
+                place_odd_rows(nc.sync, k2_plane, k2_bytes, 0)
             h.append(keep.tile([P, 2 * S], F32, name="h%d" % t))
-            nc.vector.tensor_scalar(h[t][:, :S], acc[:], SIXTEENTH, None, ALU.mult, ALU.min, accum_out=low[:, col])
-            nc.vector.tensor_tensor(exp_bias[:, col], low[:, col], tau_t[:, col], ALU.mult)
-            ea.append(keep.tile([P, S], F32, name="ea%d" % t))
+            nc.vector.tensor_scalar(h[t][:, :S], h_sums[t][:], SIXTEENTH, None, ALU.mult, ALU.min, accum_out=low[:, col])
+            nc.gpsimd.tensor_tensor(exp_bias[:, col], low[:, col], tau_t[:, col], ALU.mult)
+            ea.append(keep.tile([P, S], F32, name="ea%d" % t, align_bytes=64))
             h_n2.append(keep.tile([P, S], F32, name="h_n2_%d" % t))
             nc.scalar.activation(
                 ea[t][:], h[t][:].indirect(n1_t[:]), ACT.Exp, bias=exp_bias[:, col], scale=neg_tau[:, col]
             )
             nc.scalar.activation(h_n2[t][:], h[t][:].indirect(n2_t[:]), ACT.Copy, scale=-2.0)
 
-        sig_bias = keep.tile([P, TILES], F32, name="sig_bias", tag="bias")
-        nc.vector.scalar_tensor_tensor(sig_bias[:], sl_t, -1.0, th_t, ALU.mult, ALU.mult)
+        k2_words = gather_words("k2_words", d_codes, k2_t[:], H, "lhs_words")
+        two_bytes = gather_bytes("two_bytes", x_bytes, two_t[:], S, "two_bytes")
+        two_words = gather_words("two_words", x_codes, two_t[:], S, "x_picked_words")
+        neg_th = keep.tile([P, TILES], F32, name="neg_th")
+        nc.gpsimd.tensor_scalar(neg_th[:], th_t[:], -1.0, 0.0, ALU.mult, ALU.add)
+        sig_bias = keep.tile([P, TILES], F32, name="sig_bias")
+        nc.gpsimd.tensor_tensor(sig_bias[:], sl_t[:], neg_th[:], ALU.mult)
 
-        z = keep.tile([P, TILES, S], F32, name="z")
+        z = keep.tile([P, TILES, S], F32, name="z", align_bytes=64)
         for t in range(TILES):
             col = slice(t, t + 1)
-            pull = keep.tile([P, S], F32, name="pull%d" % t)
+            pull = keep.tile([P, S], F32, name="pull%d" % t, align_bytes=64)
             nc.vector.scalar_tensor_tensor(pull[:], h_n2[t][:], gs_t[:, col], ea[t][:], ALU.mult, ALU.mult)
             nc.vector.scalar_tensor_tensor(z[:, t, :], h[t][:, :S], gs_t[:, col], pull[:], ALU.mult, ALU.add)
 
+        cand_words = [gather_words("cand_low", x_codes, cand_t[:, : C // 32], C // 2, "ea%d" % (TILES - 1))]
         z_bf = keep.tile([P, S, PACK], BF16, name="z_bf", align_bytes=64)
         nc.vector.tensor_copy(
             z_bf[:].rearrange("p (c i) t -> p c t i", i=4), z[:].rearrange("p t (c i) -> p c t i", i=4)
         )
+        cand_bytes = gather_bytes("cand_bytes", x_bytes, cand_t[:], C, "pull%d" % (TILES - 1))
         z_words = keep.tile([P, S], U32, name="z_words", align_bytes=64)
         z_bytes = keep.tile([P, S], U8, name="z_bytes", align_bytes=64)
         nc.vector.quantize_mx(
             out=z_words[:].bitcast(FP8X4), scales=z_bytes[:], in_=z_bf[:].rearrange("p j t -> p (j t)")
         )
 
-        k2_bytes = gather_bytes("k2_bytes", d_bytes, k2_t, H, "k2_bytes")
-        k2_plane = keep.tile([P, H], U8, name="k2_plane", align_bytes=64)
-        nc.vector.tensor_copy(k2_plane[:].bitcast(I32), k2_bytes[:].bitcast(I32))
-        place_odd_rows(nc.sync, k2_plane, k2_bytes)
-        k2_words = gather_words("k2_words", d_codes, k2_t, H, "lhs_words")
-        two_bytes = gather_bytes("two_bytes", x_bytes, two_t, S, "x_picked_bytes")
-        two_words = gather_words("two_words", x_codes, two_t, S, "x_picked_words")
         sg = []
         for t in range(TILES):
             col = slice(t, t + 1)
-            acc = product("bank%d" % (TILES + t), k2_words, k2_plane, t, two_words, two_bytes)
+            acc = product("bank%d" % (TILES + t), k2_words[:, block(t)], k2_plane[:, block(t)], two_words, two_bytes)
             b = keep.tile([P, 2 * S], F32, name="b%d" % t)
             nc.scalar.activation(b[:, :S], acc[:], ACT.Copy, scale=SIXTEENTH)
             sg.append(keep.tile([P, S], F32, name="sg%d" % t))
@@ -172,15 +183,19 @@ def tile_picked_pqcjgxbebz_none_p_kernel(
                 sg[t][:], b[:].indirect(n3_t[:]), ACT.Sigmoid, bias=sig_bias[:, col], scale=sl_t[:, col]
             )
 
-        cand_bytes = gather_bytes("cand_bytes", x_bytes, cand_t, C, "lhs_bytes")
-        cand_words = gather_words("cand_words", x_codes, cand_t, C, "x_picked_words")
+        cand_words.append(gather_words("cand_high", x_codes, cand_t[:, C // 32 :], C // 2, "z"))
         neg_half_a, gated = [], []
         for t in range(TILES):
-            acc = product("bank%d" % t, cand_words, cand_bytes, t, z_words, z_bytes)
+            acc = product("bank%d" % (TILES + t), cand_words[t // 2][:, block(t % 2)], cand_bytes[:, block(t)], z_words, z_bytes)
             gated.append(keep.tile([P, S], F32, name="gated%d" % t))
-            nc.vector.scalar_tensor_tensor(gated[t][:], acc[:], SIXTEENTH, sg[t][:], ALU.mult, ALU.mult)
             neg_half_a.append(keep.tile([P, 2 * S], F32, name="neg_half_a%d" % t))
-            nc.scalar.activation(neg_half_a[t][:, :S], acc[:], ACT.Copy, scale=-0.5 * SIXTEENTH)
+            if t >= TILES // 2:
+                nc.scalar.activation(neg_half_a[t][:, :S], acc[:], ACT.Copy, scale=-0.5 * SIXTEENTH)
+            nc.vector.scalar_tensor_tensor(gated[t][:], acc[:], SIXTEENTH, sg[t][:], ALU.mult, ALU.mult)
+            if t == 0:
+                nc.vector.tensor_scalar(neg_half_a[t][:, :S], acc[:], -0.5 * SIXTEENTH, None, ALU.mult)
+            elif t < TILES // 2:
+                nc.scalar.activation(neg_half_a[t][:, :S], acc[:], ACT.Copy, scale=-0.5 * SIXTEENTH)
         for t in range(TILES):
             res = keep.tile([P, S], F32, name="res%d" % t)
             if t < TILES // 2:

@@ -67,12 +67,12 @@ def tile_picked_pqcjgxbebz_none_p_kernel(
         tau_t = load_column("tau_t", tau.rearrange("(p t) o -> p (t o)", t=PACK))
         n1_t = load_list("n1_t", n1)
         n2_t = load_list("n2_t", n2)
-        gs_t = load_column("gs_t", gs.rearrange("(p t) o -> p (t o)", t=PACK))
-        cand_t = load_list("cand_t", cand)
-        n3_t = load_list("n3_t", n3)
         with nc.allow_non_contiguous_dma(reason="one value a row and partition"):
             sl_t = load_column("sl_t", sl.rearrange("(t p) o -> p (t o)", p=P))
             th_t = load_column("th_t", th.rearrange("(t p) o -> p (t o)", p=P))
+        gs_t = load_column("gs_t", gs.rearrange("(p t) o -> p (t o)", t=PACK))
+        cand_t = load_list("cand_t", cand)
+        n3_t = load_list("n3_t", n3)
         n4_t = load_list("n4_t", n4)
 
         def gather_words(name, table, offsets, n, tag):
@@ -108,7 +108,8 @@ def tile_picked_pqcjgxbebz_none_p_kernel(
         k1_bytes = gather_bytes("k1_bytes", d_bytes, k1_t[:], H, "k1_bytes")
         k1_plane = keep.tile([P, H], U8, name="k1_plane", tag="lhs_bytes", align_bytes=64)
         nc.vector.tensor_copy(
-            k1_plane[:].rearrange("p (t m) -> p t m", t=PACK), k1_bytes[:].rearrange("p (m t) -> p t m", t=PACK)
+            k1_plane[:].rearrange("p (t c i) -> p c t i", t=PACK, i=16),
+            k1_bytes[:].rearrange("p (c i t) -> p c t i", t=PACK, i=16),
         )
         place_odd_rows(nc.scalar, k1_plane, k1_plane, 1)
         offs_bytes = gather_bytes("offs_bytes", x_bytes, offs_t[:], S, "x_picked_bytes")
@@ -116,8 +117,8 @@ def tile_picked_pqcjgxbebz_none_p_kernel(
         offs_words = gather_words("offs_words", x_codes, offs_t[:], S, "x_picked_words")
         k1_dealt = keep.tile([P, H], U32, name="k1_dealt", tag="lhs_words", align_bytes=64)
         nc.vector.tensor_copy(
-            k1_dealt[:].bitcast(I32).rearrange("p (t m) -> p t m", t=PACK),
-            k1_words[:].bitcast(I32).rearrange("p (m t) -> p t m", t=PACK),
+            k1_dealt[:].bitcast(I32).rearrange("p (t c i) -> p c t i", t=PACK, i=4),
+            k1_words[:].bitcast(I32).rearrange("p (c i t) -> p c t i", t=PACK, i=4),
         )
 
         neg_tau = keep.tile([P, TILES], F32, name="neg_tau")
@@ -137,7 +138,7 @@ def tile_picked_pqcjgxbebz_none_p_kernel(
                 place_odd_rows(nc.sync, k2_plane, k2_bytes, 0)
             h.append(keep.tile([P, 2 * S], F32, name="h%d" % t))
             nc.vector.tensor_scalar(h[t][:, :S], h_sums[t][:], SIXTEENTH, None, ALU.mult, ALU.min, accum_out=low[:, col])
-            nc.gpsimd.tensor_tensor(exp_bias[:, col], low[:, col], tau_t[:, col], ALU.mult)
+            nc.vector.tensor_tensor(exp_bias[:, col], low[:, col], tau_t[:, col], ALU.mult)
             ea.append(keep.tile([P, S], F32, name="ea%d" % t, align_bytes=64))
             h_n2.append(keep.tile([P, S], F32, name="h_n2_%d" % t))
             nc.scalar.activation(
@@ -148,10 +149,8 @@ def tile_picked_pqcjgxbebz_none_p_kernel(
         k2_words = gather_words("k2_words", d_codes, k2_t[:], H, "lhs_words")
         two_bytes = gather_bytes("two_bytes", x_bytes, two_t[:], S, "two_bytes")
         two_words = gather_words("two_words", x_codes, two_t[:], S, "x_picked_words")
-        neg_th = keep.tile([P, TILES], F32, name="neg_th")
-        nc.gpsimd.tensor_scalar(neg_th[:], th_t[:], -1.0, 0.0, ALU.mult, ALU.add)
         sig_bias = keep.tile([P, TILES], F32, name="sig_bias")
-        nc.gpsimd.tensor_tensor(sig_bias[:], sl_t[:], neg_th[:], ALU.mult)
+        nc.vector.scalar_tensor_tensor(sig_bias[:], sl_t[:], -1.0, th_t[:], ALU.mult, ALU.mult)
 
         z = keep.tile([P, TILES, S], F32, name="z", align_bytes=64)
         for t in range(TILES):

from contextlib import ExitStack

import concourse.mybir as mybir

K, T, S, G, H, C = 512, 1024, 256, 2048, 512, 512
FLOPS = 2 * K * S * (H + C + H)

F32 = mybir.dt.float32
BF16 = mybir.dt.bfloat16
I32 = mybir.dt.int32
U32 = mybir.dt.uint32
U16 = mybir.dt.uint16
U8 = mybir.dt.uint8
FP8X4 = mybir.dt.float8_e4m3fn_x4
ALU = mybir.AluOpType
ACT = mybir.ActivationFunctionType

P = 128
PACK = 4
TILES = H // P
SIXTEENTH = 0.0625


def tile_picked_pqcjgxbebz_none_p_kernel(
    tc, x_words, x_scales, d_words, d_scales, tau, gs, sl, th, offs, k1, n1, n2, cand, two, k2, n3, n4, out
):
    nc = tc.nc
    with ExitStack() as ctx:
        keep = ctx.enter_context(tc.tile_pool(name="keep", bufs=1))
        psum = ctx.enter_context(tc.psum_pool(name="psum", bufs=1))

        def load_list(name, src):
            tile = keep.tile(list(src.shape), U16, name=name)
            nc.sync.dma_start(tile[:], src)
            return tile

        d_bytes = keep.tile([P, G], U8, name="d_bytes", align_bytes=64)
        x_bytes = keep.tile([P, T], U8, name="x_bytes", align_bytes=64)
        nc.vector.memset(d_bytes[:].bitcast(I32), 0)
        nc.gpsimd.memset(x_bytes[:].bitcast(I32), 0)
        k2_plane = keep.tile([P, H], U8, name="k2_plane", align_bytes=64)
        nc.vector.memset(k2_plane[:].bitcast(I32), 0)
        d_rows = d_scales[0].bitcast(I32)
        x_rows = x_scales[0].bitcast(I32)

        def load_x_rows(q):
            nc.sync.dma_start(x_bytes[:].bitcast(I32)[32 * q : 32 * q + 4, :], x_rows[4 * q : 4 * q + 4, :])

        def load_column(name, src):
            tile = keep.tile([P, TILES], F32, name=name)
            nc.sync.dma_start(tile[:], src)
            return tile

        k1_t = load_list("k1_t", k1)
        offs_t = load_list("offs_t", offs)
        load_x_rows(0)
        load_x_rows(1)
        nc.sync.dma_start(d_bytes[:].bitcast(I32)[0:P:8, :], d_rows)
        load_x_rows(2)
        load_x_rows(3)
        d_codes = keep.tile([P, G], I32, name="d_codes", align_bytes=64)
        nc.sync.dma_start(d_codes[:], d_words[0].rearrange("p n t -> p (n t)").bitcast(I32))
        k2_t = load_list("k2_t", k2)
        x_codes = keep.tile([P, T], I32, name="x_codes", align_bytes=64)
        nc.sync.dma_start(x_codes[:], x_words[0].rearrange("p n t -> p (n t)").bitcast(I32))
        two_t = load_list("two_t", two)
        tau_t = load_column("tau_t", tau.rearrange("(p t) o -> p (t o)", t=PACK))
        n1_t = load_list("n1_t", n1)
        n2_t = load_list("n2_t", n2)
        with nc.allow_non_contiguous_dma(reason="one value a row and partition"):
            sl_t = load_column("sl_t", sl.rearrange("(t p) o -> p (t o)", p=P))
            th_t = load_column("th_t", th.rearrange("(t p) o -> p (t o)", p=P))
        gs_t = load_column("gs_t", gs.rearrange("(p t) o -> p (t o)", t=PACK))
        cand_t = load_list("cand_t", cand)
        n3_t = load_list("n3_t", n3)
        n4_t = load_list("n4_t", n4)

        def gather_words(name, table, offsets, n, tag):
            tile = keep.tile([P, n], U32, name=name, tag=tag, align_bytes=64)
            nc.vector.tensor_copy(tile[:], table[:].bitcast(U32).indirect(offsets))
            return tile

        def gather_bytes(name, table, offsets, n, tag):
            tile = keep.tile([P, n], U8, name=name, tag=tag, align_bytes=64)
            nc.vector.tensor_copy(tile[:], table[:].indirect(offsets))
            return tile

        def place_odd_rows(queue, dst, src, first):
            for c in range(first, 4):
                queue.dma_start(dst[:].bitcast(I32)[c:P:32, :], src[:].bitcast(I32)[8 * c : P : 32, :])

        def block(t):
            return slice(t * P, (t + 1) * P)

        def product(tag, lhs_words, lhs_bytes, rhs_words, rhs_bytes):
            acc = psum.tile([P, S], F32, name="acc", tag=tag)
            nc.tensor.matmul_mx(
                out=acc[:],
                lhsT=lhs_words.bitcast(FP8X4),
                lhsT_scale=lhs_bytes,
                rhs=rhs_words[:].bitcast(FP8X4),
                rhs_scale=rhs_bytes[:],
                start=True,
                stop=True,
            )
            return acc

        k1_bytes = gather_bytes("k1_bytes", d_bytes, k1_t[:], H, "k1_bytes")
        k1_plane = keep.tile([P, H], U8, name="k1_plane", tag="lhs_bytes", align_bytes=64)
        nc.vector.tensor_copy(
            k1_plane[:].rearrange("p (t c i) -> p c t i", t=PACK, i=16),
            k1_bytes[:].rearrange("p (c i t) -> p c t i", t=PACK, i=16),
        )
        place_odd_rows(nc.scalar, k1_plane, k1_plane, 1)
        offs_bytes = gather_bytes("offs_bytes", x_bytes, offs_t[:], S, "x_picked_bytes")
        k1_words = gather_words("k1_words", d_codes, k1_t[:], H, "k1_words")
        offs_words = gather_words("offs_words", x_codes, offs_t[:], S, "x_picked_words")
        k1_dealt = keep.tile([P, H], U32, name="k1_dealt", tag="lhs_words", align_bytes=64)
        nc.vector.tensor_copy(
            k1_dealt[:].bitcast(I32).rearrange("p (t c i) -> p c t i", t=PACK, i=4),
            k1_words[:].bitcast(I32).rearrange("p (c i t) -> p c t i", t=PACK, i=4),
        )

        neg_tau = keep.tile([P, TILES], F32, name="neg_tau")
        nc.scalar.activation(neg_tau[:], tau_t[:], ACT.Copy, scale=-1.0)

        low = keep.tile([P, TILES], F32, name="low")
        exp_bias = keep.tile([P, TILES], F32, name="exp_bias")
        h, ea, h_n2 = [], [], []
        h_sums = [
            product("bank%d" % t, k1_dealt[:, block(t)], k1_plane[:, block(t)], offs_words, offs_bytes)
            for t in range(TILES)
        ]
        for t in range(TILES):
            col = slice(t, t + 1)
            if t == TILES // 2:
                k2_bytes = gather_bytes("k2_bytes", d_bytes, k2_t[:], H, "lhs_bytes")
                place_odd_rows(nc.sync, k2_plane, k2_bytes, 0)
            h.append(keep.tile([P, 2 * S], F32, name="h%d" % t))
            nc.vector.tensor_scalar(h[t][:, :S], h_sums[t][:], SIXTEENTH, None, ALU.mult, ALU.min, accum_out=low[:, col])
            nc.vector.tensor_tensor(exp_bias[:, col], low[:, col], tau_t[:, col], ALU.mult)
            ea.append(keep.tile([P, S], F32, name="ea%d" % t, align_bytes=64))
            h_n2.append(keep.tile([P, S], F32, name="h_n2_%d" % t))
            nc.scalar.activation(
                ea[t][:], h[t][:].indirect(n1_t[:]), ACT.Exp, bias=exp_bias[:, col], scale=neg_tau[:, col]
            )
            nc.scalar.activation(h_n2[t][:], h[t][:].indirect(n2_t[:]), ACT.Copy, scale=-2.0)

        k2_words = gather_words("k2_words", d_codes, k2_t[:], H, "lhs_words")
        two_bytes = gather_bytes("two_bytes", x_bytes, two_t[:], S, "two_bytes")
        two_words = gather_words("two_words", x_codes, two_t[:], S, "x_picked_words")
        sig_bias = keep.tile([P, TILES], F32, name="sig_bias")
        nc.vector.scalar_tensor_tensor(sig_bias[:], sl_t[:], -1.0, th_t[:], ALU.mult, ALU.mult)

        z = keep.tile([P, TILES, S], F32, name="z", align_bytes=64)
        for t in range(TILES):
            col = slice(t, t + 1)
            pull = keep.tile([P, S], F32, name="pull%d" % t, align_bytes=64)
            nc.vector.scalar_tensor_tensor(pull[:], h_n2[t][:], gs_t[:, col], ea[t][:], ALU.mult, ALU.mult)
            nc.vector.scalar_tensor_tensor(z[:, t, :], h[t][:, :S], gs_t[:, col], pull[:], ALU.mult, ALU.add)

        cand_words = [gather_words("cand_low", x_codes, cand_t[:, : C // 32], C // 2, "ea%d" % (TILES - 1))]
        z_bf = keep.tile([P, S, PACK], BF16, name="z_bf", align_bytes=64)
        nc.vector.tensor_copy(
            z_bf[:].rearrange("p (c i) t -> p c t i", i=4), z[:].rearrange("p t (c i) -> p c t i", i=4)
        )
        cand_bytes = gather_bytes("cand_bytes", x_bytes, cand_t[:], C, "pull%d" % (TILES - 1))
        z_words = keep.tile([P, S], U32, name="z_words", align_bytes=64)
        z_bytes = keep.tile([P, S], U8, name="z_bytes", align_bytes=64)
        nc.vector.quantize_mx(
            out=z_words[:].bitcast(FP8X4), scales=z_bytes[:], in_=z_bf[:].rearrange("p j t -> p (j t)")
        )

        sg = []
        for t in range(TILES):
            col = slice(t, t + 1)
            acc = product("bank%d" % (TILES + t), k2_words[:, block(t)], k2_plane[:, block(t)], two_words, two_bytes)
            b = keep.tile([P, 2 * S], F32, name="b%d" % t)
            nc.scalar.activation(b[:, :S], acc[:], ACT.Copy, scale=SIXTEENTH)
            sg.append(keep.tile([P, S], F32, name="sg%d" % t))
            nc.scalar.activation(
                sg[t][:], b[:].indirect(n3_t[:]), ACT.Sigmoid, bias=sig_bias[:, col], scale=sl_t[:, col]
            )

        cand_words.append(gather_words("cand_high", x_codes, cand_t[:, C // 32 :], C // 2, "z"))
        neg_half_a, gated = [], []
        for t in range(TILES):
            acc = product("bank%d" % (TILES + t), cand_words[t // 2][:, block(t % 2)], cand_bytes[:, block(t)], z_words, z_bytes)
            gated.append(keep.tile([P, S], F32, name="gated%d" % t))
            neg_half_a.append(keep.tile([P, 2 * S], F32, name="neg_half_a%d" % t))
            if t >= TILES // 2:
                nc.scalar.activation(neg_half_a[t][:, :S], acc[:], ACT.Copy, scale=-0.5 * SIXTEENTH)
            nc.vector.scalar_tensor_tensor(gated[t][:], acc[:], SIXTEENTH, sg[t][:], ALU.mult, ALU.mult)
            if t == 0:
                nc.vector.tensor_scalar(neg_half_a[t][:, :S], acc[:], -0.5 * SIXTEENTH, None, ALU.mult)
            elif t < TILES // 2:
                nc.scalar.activation(neg_half_a[t][:, :S], acc[:], ACT.Copy, scale=-0.5 * SIXTEENTH)
        for t in range(TILES):
            res = keep.tile([P, S], F32, name="res%d" % t)
            if t < TILES // 2:
                nc.vector.tensor_tensor(res[:], neg_half_a[t][:].indirect(n4_t[:]), gated[t][:], ALU.add)
            else:
                fetched = keep.tile([P, S], F32, name="fetched%d" % t)
                nc.scalar.activation(fetched[:], neg_half_a[t][:].indirect(n4_t[:]), ACT.Copy)
                nc.vector.tensor_tensor(res[:], fetched[:], gated[t][:], ALU.add)
            nc.sync.dma_start(out[t * P : (t + 1) * P, :], res[:])
